import numpy as np
import ml_dtypes


def mxq(x, axis, fmt="e4m3"):
    dtype, down = {"e4m3": (ml_dtypes.float8_e4m3fn, 7), "e5m2": (ml_dtypes.float8_e5m2, 14)}[fmt]
    v = np.moveaxis(np.asarray(x, np.float32).astype(ml_dtypes.bfloat16).astype(np.float64), axis, -1)
    blocks = v.reshape(v.shape[:-1] + (-1, 32))
    amax = np.abs(blocks).max(-1, keepdims=True)
    byte = np.maximum(np.where(amax > 0, np.frexp(amax)[1] - 1 + 127, 0) - down, 1)
    scale = np.exp2(byte - 127.0)
    codes = (blocks / scale).astype(np.float32).astype(dtype).astype(np.float64)
    return np.moveaxis((codes * scale).reshape(v.shape), -1, axis)


WIDE = False


def mx_kscale(k):
    if not WIDE:
        return np.ones(k)
    levels = np.array([10, -10, 5, -5, 0])
    if k % 512:
        return np.exp2(np.random.permutation(np.resize(levels, k // 32))).repeat(32)
    a = np.empty((k // 512, 16))
    for p in range(k // 512):
        a[p, :8] = np.random.permutation(np.resize(levels, 8))
        for g in range(8):
            far = levels[np.abs(levels - a[p, g]) >= 10]
            a[p, g + 8] = far[np.random.randint(len(far))]
    return np.exp2(a.ravel()).repeat(32)


def f64(x):
    return np.asarray(x).astype(np.float64)


def striped(idx):
    return np.tile(idx.reshape(-1, 16).T, (8, 1)).astype(np.uint16)


def unstriped(offs):
    return offs[:16].T.reshape(-1).astype(np.int64)


def pack_weight(w):
    k, n = w.shape
    w = f64(np.asarray(w, np.float32).astype(ml_dtypes.bfloat16)).reshape(k // 32, 32, n)
    amax = np.abs(w).max(1)
    byte = np.clip(np.where(amax > 0, np.frexp(amax)[1] - 1 + 127 - 7, 1), 1, 254)
    scaled = (w * np.exp2(127.0 - byte)[:, None, :]).reshape(k, n).astype(np.float32)
    words = np.ascontiguousarray(scaled.reshape(k // 512, 128, 4, n).transpose(0, 1, 3, 2)).astype(ml_dtypes.float8_e4m3fn).view(np.uint8)
    return words, np.ascontiguousarray(byte.astype(np.uint8).reshape(k // 512, 16, n))


def unpack_weight(words, scales):
    g, p, n, _ = words.shape
    vals = np.ascontiguousarray(words).view(ml_dtypes.float8_e4m3fn).astype(np.float64) * np.repeat(np.exp2(scales.astype(np.float64) - 127.0), 8, axis=1)[..., None]
    return vals.transpose(0, 1, 3, 2).reshape(g * 512, n)


K, T, N, U = 1024, 512, 128, 1024


def setup_inputs():
    n = np.random.standard_normal
    s = mx_kscale(K)[:, None]
    packed_xT = pack_weight(n((K, T)) * s)
    return {
        "x_words": packed_xT[0],
        "x_scales": packed_xT[1],
        "mem": n((N, U)).astype(np.float32),
        "w1": (n((K, N)) / np.sqrt(K) / s).astype(np.float32),
        "slot": striped(np.random.permutation(U)[:T]),
    }


def reference(x_words, x_scales, mem, w1, slot):
    xq = unpack_weight(x_words, x_scales)
    y = mxq(f64(w1), 0, "e4m3").T @ xq
    out = f64(mem).copy()
    out[:, unstriped(slot)] = y
    return out

@@ -1,0 +1,90 @@
+from contextlib import ExitStack
+
+import concourse.mybir as mybir
+
+K, T, N, U = 1024, 512, 128, 1024
+FLOPS = 2 * K * T * N
+
+F32 = mybir.dt.float32
+BF16 = mybir.dt.bfloat16
+I32 = mybir.dt.int32
+U32 = mybir.dt.uint32
+U16 = mybir.dt.uint16
+U8 = mybir.dt.uint8
+FP8X4 = mybir.dt.float8_e4m3fn_x4
+
+P = 128
+PACK = 4
+K_PASS = P * PACK
+PASSES = K // K_PASS
+LOADS = [(0, 256), (256, 512)]
+CHUNKS = [(0, 128), (128, 256), (256, 512)]
+
+
+def tile_picked_wkvput_none_l_kernel(tc, x_words, x_scales, mem, w1, slot, out):
+    nc = tc.nc
+    with ExitStack() as ctx:
+        keep = ctx.enter_context(tc.tile_pool(name="keep", bufs=1))
+        psum = ctx.enter_context(tc.psum_pool(name="psum", bufs=1))
+
+        w_raw = []
+        for g in range(PASSES):
+            raw = keep.tile([P, PACK, N], F32, name="w_raw%d" % g)
+            nc.sync.dma_start(out=raw[:], in_=w1[g * K_PASS : (g + 1) * K_PASS, :].rearrange("(p j) m -> p j m", j=PACK))
+            w_raw.append(raw)
+
+        xs = keep.tile([P, PASSES, T], U8, name="xs", align_bytes=64)
+        for q in range(4):
+            nc.sync.dma_start(
+                out=xs[32 * q : 32 * q + 4, :, :].bitcast(I32),
+                in_=x_scales[:, 4 * q : 4 * q + 4, :].rearrange("z r c -> r z c").bitcast(I32),
+            )
+
+        words = x_words.rearrange("z p c r -> p z (c r)")
+        xw = []
+
+        def load_words(i):
+            a, b = LOADS[i]
+            t = keep.tile([P, PASSES, b - a], U32, name="xw%d" % i, align_bytes=64)
+            nc.sync.dma_start(out=t[:].bitcast(I32), in_=words[:, :, PACK * a : PACK * b].bitcast(I32))
+            xw.append(t)
+
+        load_words(0)
+        window = keep.tile([P, U], F32, name="window")
+        nc.sync.dma_start(out=window[:], in_=mem)
+        offsets = keep.tile([P, T // 16], U16, name="offsets")
+        nc.sync.dma_start(offsets[:], slot)
+        load_words(1)
+
+        w_codes, w_scales = [], []
+        for g in range(PASSES):
+            grouped = keep.tile([P, N, PACK], BF16, name="w_bf%d" % g, align_bytes=64)
+            nc.vector.tensor_copy(
+                out=grouped[:].rearrange("p (c i) t -> p c t i", i=4),
+                in_=w_raw[g][:].rearrange("p t (c i) -> p c t i", i=4),
+            )
+            codes = keep.tile([P, N], U32, name="w_codes%d" % g, align_bytes=64)
+            scales = keep.tile([P, N], U8, name="w_scales%d" % g, align_bytes=64)
+            nc.vector.quantize_mx(out=codes[:].bitcast(FP8X4), scales=scales[:], in_=grouped[:].rearrange("p m j -> p (m j)"))
+            w_codes.append(codes)
+            w_scales.append(scales)
+
+        for c, (a, b) in enumerate(CHUNKS):
+            i = [n for n, (la, lb) in enumerate(LOADS) if la <= a and b <= lb][0]
+            la = LOADS[i][0]
+            acc = psum.tile([P, b - a], F32, name="acc%d" % c)
+            for g in range(PASSES):
+                nc.tensor.matmul_mx(
+                    out=acc[:],
+                    lhsT=w_codes[g][:].bitcast(FP8X4),
+                    lhsT_scale=w_scales[g][:],
+                    rhs=xw[i][:, g, a - la : b - la].bitcast(FP8X4),
+                    rhs_scale=xs[:, g, a:b],
+                    start=(g == 0),
+                    stop=(g == PASSES - 1),
+                )
+            y = keep.tile([P, b - a], F32, name="y%d" % c)
+            nc.scalar.copy(out=y[:], in_=acc[:])
+            nc.vector.tensor_copy(window[:].indirect(offsets[:, a // 16 : b // 16]), y[:])
+
+        nc.sync.dma_start(out=out, in_=window[:])

@@ -17,8 +17,8 @@ P = 128
 PACK = 4
 K_PASS = P * PACK
 PASSES = K // K_PASS
-LOADS = [(0, 256), (256, 512)]
-CHUNKS = [(0, 128), (128, 256), (256, 512)]
+HALF = T // 2
+COLS = 128
 
 
 def tile_picked_wkvput_none_l_kernel(tc, x_words, x_scales, mem, w1, slot, out):
@@ -34,57 +34,56 @@ def tile_picked_wkvput_none_l_kernel(tc, x_words, x_scales, mem, w1, slot, out):
             w_raw.append(raw)
 
         xs = keep.tile([P, PASSES, T], U8, name="xs", align_bytes=64)
-        for q in range(4):
+        for r in range(4):
             nc.sync.dma_start(
-                out=xs[32 * q : 32 * q + 4, :, :].bitcast(I32),
-                in_=x_scales[:, 4 * q : 4 * q + 4, :].rearrange("z r c -> r z c").bitcast(I32),
+                out=xs[r:P:32, :, :].bitcast(I32),
+                in_=x_scales[:, r:16:4, :].rearrange("z q c -> q z c").bitcast(I32),
             )
 
         words = x_words.rearrange("z p c r -> p z (c r)")
-        xw = []
-
-        def load_words(i):
-            a, b = LOADS[i]
-            t = keep.tile([P, PASSES, b - a], U32, name="xw%d" % i, align_bytes=64)
-            nc.sync.dma_start(out=t[:].bitcast(I32), in_=words[:, :, PACK * a : PACK * b].bitcast(I32))
-            xw.append(t)
-
-        load_words(0)
+        early = keep.tile([P, PASSES, HALF], U32, name="early", align_bytes=64)
+        nc.sync.dma_start(out=early[:].bitcast(I32), in_=words[:, :, 0 : PACK * HALF].bitcast(I32))
         window = keep.tile([P, U], F32, name="window")
         nc.sync.dma_start(out=window[:], in_=mem)
         offsets = keep.tile([P, T // 16], U16, name="offsets")
         nc.sync.dma_start(offsets[:], slot)
-        load_words(1)
+        late = []
+        for g in range(PASSES):
+            t = keep.tile([P, HALF], U32, name="late%d" % g, align_bytes=64)
+            nc.sync.dma_start(out=t[:].bitcast(I32), in_=words[:, g, PACK * HALF : PACK * T].bitcast(I32))
+            late.append(t)
+        x_codes = [[early[:, g, :] for g in range(PASSES)], [late[g][:] for g in range(PASSES)]]
 
         w_codes, w_scales = [], []
         for g in range(PASSES):
             grouped = keep.tile([P, N, PACK], BF16, name="w_bf%d" % g, align_bytes=64)
-            nc.vector.tensor_copy(
-                out=grouped[:].rearrange("p (c i) t -> p c t i", i=4),
-                in_=w_raw[g][:].rearrange("p t (c i) -> p c t i", i=4),
-            )
+            dst = grouped[:].rearrange("p (c i) t -> p c t i", i=4)
+            src = w_raw[g][:].rearrange("p t (c i) -> p c t i", i=4)
+            nc.vector.tensor_copy(out=dst[:, 0:18], in_=src[:, 0:18])
+            nc.scalar.copy(out=dst[:, 18:32], in_=src[:, 18:32])
             codes = keep.tile([P, N], U32, name="w_codes%d" % g, align_bytes=64)
             scales = keep.tile([P, N], U8, name="w_scales%d" % g, align_bytes=64)
             nc.vector.quantize_mx(out=codes[:].bitcast(FP8X4), scales=scales[:], in_=grouped[:].rearrange("p m j -> p (m j)"))
             w_codes.append(codes)
             w_scales.append(scales)
 
-        for c, (a, b) in enumerate(CHUNKS):
-            i = [n for n, (la, lb) in enumerate(LOADS) if la <= a and b <= lb][0]
-            la = LOADS[i][0]
-            acc = psum.tile([P, b - a], F32, name="acc%d" % c)
+        for h in range(2):
+            y = keep.tile([P, HALF], F32, name="y%d" % h)
+            accs = [psum.tile([P, COLS], F32, name="acc%d_%d" % (h, c)) for c in range(HALF // COLS)]
             for g in range(PASSES):
-                nc.tensor.matmul_mx(
-                    out=acc[:],
-                    lhsT=w_codes[g][:].bitcast(FP8X4),
-                    lhsT_scale=w_scales[g][:],
-                    rhs=xw[i][:, g, a - la : b - la].bitcast(FP8X4),
-                    rhs_scale=xs[:, g, a:b],
-                    start=(g == 0),
-                    stop=(g == PASSES - 1),
-                )
-            y = keep.tile([P, b - a], F32, name="y%d" % c)
-            nc.scalar.copy(out=y[:], in_=acc[:])
-            nc.vector.tensor_copy(window[:].indirect(offsets[:, a // 16 : b // 16]), y[:])
+                for c, acc in enumerate(accs):
+                    a = c * COLS
+                    nc.tensor.matmul_mx(
+                        out=acc[:],
+                        lhsT=w_codes[g][:].bitcast(FP8X4),
+                        lhsT_scale=w_scales[g][:],
+                        rhs=x_codes[h][g][:, a : a + COLS].bitcast(FP8X4),
+                        rhs_scale=xs[:, g, h * HALF + a : h * HALF + a + COLS],
+                        start=(g == 0),
+                        stop=(g == PASSES - 1),
+                    )
+            for c, acc in enumerate(accs):
+                nc.scalar.copy(out=y[:, c * COLS : (c + 1) * COLS], in_=acc[:])
+            nc.vector.tensor_copy(window[:].indirect(offsets[:, h * HALF // 16 : (h + 1) * HALF // 16]), y[:])
 
         nc.sync.dma_start(out=out, in_=window[:])

@@ -86,4 +86,5 @@ def tile_picked_wkvput_none_l_kernel(tc, x_words, x_scales, mem, w1, slot, out):
                 nc.scalar.copy(out=y[:, c * COLS : (c + 1) * COLS], in_=acc[:])
             nc.vector.tensor_copy(window[:].indirect(offsets[:, h * HALF // 16 : (h + 1) * HALF // 16]), y[:])
 
-        nc.sync.dma_start(out=out, in_=window[:])
+        nc.sync.dma_start(out=out[:, 0 : U // 2], in_=window[:, 0 : U // 2])
+        nc.scalar.dma_start(out=out[:, U // 2 : U], in_=window[:, U // 2 : U])

@@ -33,12 +33,16 @@ def tile_picked_wkvput_none_l_kernel(tc, x_words, x_scales, mem, w1, slot, out):
             nc.sync.dma_start(out=raw[:], in_=w1[g * K_PASS : (g + 1) * K_PASS, :].rearrange("(p j) m -> p j m", j=PACK))
             w_raw.append(raw)
 
-        xs = keep.tile([P, PASSES, T], U8, name="xs", align_bytes=64)
-        for r in range(4):
-            nc.sync.dma_start(
-                out=xs[r:P:32, :, :].bitcast(I32),
-                in_=x_scales[:, r:16:4, :].rearrange("z q c -> q z c").bitcast(I32),
-            )
+        def load_scales(h):
+            plane = keep.tile([P, PASSES, HALF], U8, name="xs%d" % h, align_bytes=64)
+            for r in range(4):
+                nc.sync.dma_start(
+                    out=plane[r:P:32, :, :].bitcast(I32),
+                    in_=x_scales[:, r:16:4, h * HALF : (h + 1) * HALF].rearrange("z q c -> q z c").bitcast(I32),
+                )
+            return plane
+
+        xs = [load_scales(0)]
 
         words = x_words.rearrange("z p c r -> p z (c r)")
         early = keep.tile([P, PASSES, HALF], U32, name="early", align_bytes=64)
@@ -47,6 +51,7 @@ def tile_picked_wkvput_none_l_kernel(tc, x_words, x_scales, mem, w1, slot, out):
         nc.sync.dma_start(out=window[:], in_=mem)
         offsets = keep.tile([P, T // 16], U16, name="offsets")
         nc.sync.dma_start(offsets[:], slot)
+        xs.append(load_scales(1))
         late = []
         for g in range(PASSES):
             t = keep.tile([P, HALF], U32, name="late%d" % g, align_bytes=64)
@@ -59,8 +64,8 @@ def tile_picked_wkvput_none_l_kernel(tc, x_words, x_scales, mem, w1, slot, out):
             grouped = keep.tile([P, N, PACK], BF16, name="w_bf%d" % g, align_bytes=64)
             dst = grouped[:].rearrange("p (c i) t -> p c t i", i=4)
             src = w_raw[g][:].rearrange("p t (c i) -> p c t i", i=4)
-            nc.vector.tensor_copy(out=dst[:, 0:18], in_=src[:, 0:18])
-            nc.scalar.copy(out=dst[:, 18:32], in_=src[:, 18:32])
+            nc.vector.tensor_copy(out=dst[:, 0:16], in_=src[:, 0:16])
+            nc.scalar.copy(out=dst[:, 16:32], in_=src[:, 16:32])
             codes = keep.tile([P, N], U32, name="w_codes%d" % g, align_bytes=64)
             scales = keep.tile([P, N], U8, name="w_scales%d" % g, align_bytes=64)
             nc.vector.quantize_mx(out=codes[:].bitcast(FP8X4), scales=scales[:], in_=grouped[:].rearrange("p m j -> p (m j)"))
@@ -78,12 +83,15 @@ def tile_picked_wkvput_none_l_kernel(tc, x_words, x_scales, mem, w1, slot, out):
                         lhsT=w_codes[g][:].bitcast(FP8X4),
                         lhsT_scale=w_scales[g][:],
                         rhs=x_codes[h][g][:, a : a + COLS].bitcast(FP8X4),
-                        rhs_scale=xs[:, g, h * HALF + a : h * HALF + a + COLS],
+                        rhs_scale=xs[h][:, g, a : a + COLS],
                         start=(g == 0),
                         stop=(g == PASSES - 1),
                     )
             for c, acc in enumerate(accs):
-                nc.scalar.copy(out=y[:, c * COLS : (c + 1) * COLS], in_=acc[:])
+                if h == 0 and c == 0:
+                    nc.vector.tensor_copy(out=y[:, 0:COLS], in_=acc[:])
+                else:
+                    nc.scalar.copy(out=y[:, c * COLS : (c + 1) * COLS], in_=acc[:])
             nc.vector.tensor_copy(window[:].indirect(offsets[:, h * HALF // 16 : (h + 1) * HALF // 16]), y[:])
 
         nc.sync.dma_start(out=out[:, 0 : U // 2], in_=window[:, 0 : U // 2])

@@ -29,12 +29,12 @@ def tile_picked_wkvput_none_l_kernel(tc, x_words, x_scales, mem, w1, slot, out):
 
         w_raw = []
         for g in range(PASSES):
-            raw = keep.tile([P, PACK, N], F32, name="w_raw%d" % g)
+            raw = keep.tile([P, PACK, N], F32, name="w_raw%d" % g, align_bytes=256)
             nc.sync.dma_start(out=raw[:], in_=w1[g * K_PASS : (g + 1) * K_PASS, :].rearrange("(p j) m -> p j m", j=PACK))
             w_raw.append(raw)
 
         def load_scales(h):
-            plane = keep.tile([P, PASSES, HALF], U8, name="xs%d" % h, align_bytes=64)
+            plane = keep.tile([P, PASSES, HALF], U8, name="xs%d" % h, align_bytes=256)
             for r in range(4):
                 nc.sync.dma_start(
                     out=plane[r:P:32, :, :].bitcast(I32),
@@ -45,35 +45,35 @@ def tile_picked_wkvput_none_l_kernel(tc, x_words, x_scales, mem, w1, slot, out):
         xs = [load_scales(0)]
 
         words = x_words.rearrange("z p c r -> p z (c r)")
-        early = keep.tile([P, PASSES, HALF], U32, name="early", align_bytes=64)
+        early = keep.tile([P, PASSES, HALF], U32, name="early", align_bytes=256)
         nc.sync.dma_start(out=early[:].bitcast(I32), in_=words[:, :, 0 : PACK * HALF].bitcast(I32))
-        window = keep.tile([P, U], F32, name="window")
+        window = keep.tile([P, U], F32, name="window", align_bytes=256)
         nc.sync.dma_start(out=window[:], in_=mem)
         offsets = keep.tile([P, T // 16], U16, name="offsets")
         nc.sync.dma_start(offsets[:], slot)
         xs.append(load_scales(1))
         late = []
         for g in range(PASSES):
-            t = keep.tile([P, HALF], U32, name="late%d" % g, align_bytes=64)
+            t = keep.tile([P, HALF], U32, name="late%d" % g, align_bytes=256)
             nc.sync.dma_start(out=t[:].bitcast(I32), in_=words[:, g, PACK * HALF : PACK * T].bitcast(I32))
             late.append(t)
         x_codes = [[early[:, g, :] for g in range(PASSES)], [late[g][:] for g in range(PASSES)]]
 
         w_codes, w_scales = [], []
         for g in range(PASSES):
-            grouped = keep.tile([P, N, PACK], BF16, name="w_bf%d" % g, align_bytes=64)
+            grouped = keep.tile([P, N, PACK], BF16, name="w_bf%d" % g, align_bytes=256)
             dst = grouped[:].rearrange("p (c i) t -> p c t i", i=4)
             src = w_raw[g][:].rearrange("p t (c i) -> p c t i", i=4)
             nc.vector.tensor_copy(out=dst[:, 0:16], in_=src[:, 0:16])
             nc.scalar.copy(out=dst[:, 16:32], in_=src[:, 16:32])
-            codes = keep.tile([P, N], U32, name="w_codes%d" % g, align_bytes=64)
-            scales = keep.tile([P, N], U8, name="w_scales%d" % g, align_bytes=64)
+            codes = keep.tile([P, N], U32, name="w_codes%d" % g, align_bytes=256)
+            scales = keep.tile([P, N], U8, name="w_scales%d" % g, align_bytes=256)
             nc.vector.quantize_mx(out=codes[:].bitcast(FP8X4), scales=scales[:], in_=grouped[:].rearrange("p m j -> p (m j)"))
             w_codes.append(codes)
             w_scales.append(scales)
 
         for h in range(2):
-            y = keep.tile([P, HALF], F32, name="y%d" % h)
+            y = keep.tile([P, HALF], F32, name="y%d" % h, align_bytes=256)
             accs = [psum.tile([P, COLS], F32, name="acc%d_%d" % (h, c)) for c in range(HALF // COLS)]
             for g in range(PASSES):
                 for c, acc in enumerate(accs):

@@ -33,16 +33,16 @@ def tile_picked_wkvput_none_l_kernel(tc, x_words, x_scales, mem, w1, slot, out):
             nc.sync.dma_start(out=raw[:], in_=w1[g * K_PASS : (g + 1) * K_PASS, :].rearrange("(p j) m -> p j m", j=PACK))
             w_raw.append(raw)
 
-        def load_scales(h):
+        def load_scales(h, queues):
             plane = keep.tile([P, PASSES, HALF], U8, name="xs%d" % h, align_bytes=256)
             for r in range(4):
-                nc.sync.dma_start(
+                queues[r].dma_start(
                     out=plane[r:P:32, :, :].bitcast(I32),
                     in_=x_scales[:, r:16:4, h * HALF : (h + 1) * HALF].rearrange("z q c -> q z c").bitcast(I32),
                 )
             return plane
 
-        xs = [load_scales(0)]
+        xs = [load_scales(0, [nc.scalar, nc.scalar, nc.scalar, nc.sync])]
 
         words = x_words.rearrange("z p c r -> p z (c r)")
         early = keep.tile([P, PASSES, HALF], U32, name="early", align_bytes=256)
@@ -51,7 +51,7 @@ def tile_picked_wkvput_none_l_kernel(tc, x_words, x_scales, mem, w1, slot, out):
         nc.sync.dma_start(out=window[:], in_=mem)
         offsets = keep.tile([P, T // 16], U16, name="offsets")
         nc.sync.dma_start(offsets[:], slot)
-        xs.append(load_scales(1))
+        xs.append(load_scales(1, [nc.sync] * 4))
         late = []
         for g in range(PASSES):
             t = keep.tile([P, HALF], U32, name="late%d" % g, align_bytes=256)

@@ -88,8 +88,8 @@ def tile_picked_wkvput_none_l_kernel(tc, x_words, x_scales, mem, w1, slot, out):
                         stop=(g == PASSES - 1),
                     )
             for c, acc in enumerate(accs):
-                if h == 0 and c == 0:
-                    nc.vector.tensor_copy(out=y[:, 0:COLS], in_=acc[:])
+                if h == 0:
+                    nc.vector.tensor_copy(out=y[:, c * COLS : (c + 1) * COLS], in_=acc[:])
                 else:
                     nc.scalar.copy(out=y[:, c * COLS : (c + 1) * COLS], in_=acc[:])
             nc.vector.tensor_copy(window[:].indirect(offsets[:, h * HALF // 16 : (h + 1) * HALF // 16]), y[:])

@@ -94,5 +94,4 @@ def tile_picked_wkvput_none_l_kernel(tc, x_words, x_scales, mem, w1, slot, out):
                     nc.scalar.copy(out=y[:, c * COLS : (c + 1) * COLS], in_=acc[:])
             nc.vector.tensor_copy(window[:].indirect(offsets[:, h * HALF // 16 : (h + 1) * HALF // 16]), y[:])
 
-        nc.sync.dma_start(out=out[:, 0 : U // 2], in_=window[:, 0 : U // 2])
-        nc.scalar.dma_start(out=out[:, U // 2 : U], in_=window[:, U // 2 : U])
+        nc.sync.dma_start(out=out, in_=window[:])

@@ -12,6 +12,7 @@ U32 = mybir.dt.uint32
 U16 = mybir.dt.uint16
 U8 = mybir.dt.uint8
 FP8X4 = mybir.dt.float8_e4m3fn_x4
+COPY = mybir.ActivationFunctionType.Copy
 
 P = 128
 PACK = 4
@@ -88,10 +89,11 @@ def tile_picked_wkvput_none_l_kernel(tc, x_words, x_scales, mem, w1, slot, out):
                         stop=(g == PASSES - 1),
                     )
             for c, acc in enumerate(accs):
-                if h == 0:
-                    nc.vector.tensor_copy(out=y[:, c * COLS : (c + 1) * COLS], in_=acc[:])
-                else:
-                    nc.scalar.copy(out=y[:, c * COLS : (c + 1) * COLS], in_=acc[:])
-            nc.vector.tensor_copy(window[:].indirect(offsets[:, h * HALF // 16 : (h + 1) * HALF // 16]), y[:])
+                nc.vector.tensor_copy(out=y[:, c * COLS : (c + 1) * COLS], in_=acc[:])
+            target = window[:].indirect(offsets[:, h * HALF // 16 : (h + 1) * HALF // 16])
+            if h == 0:
+                nc.scalar.activation(target, y[:], COPY)
+            else:
+                nc.vector.tensor_copy(target, y[:])
 
         nc.sync.dma_start(out=out, in_=window[:])

@@ -89,7 +89,10 @@ def tile_picked_wkvput_none_l_kernel(tc, x_words, x_scales, mem, w1, slot, out):
                         stop=(g == PASSES - 1),
                     )
             for c, acc in enumerate(accs):
-                nc.vector.tensor_copy(out=y[:, c * COLS : (c + 1) * COLS], in_=acc[:])
+                if h == 0:
+                    nc.scalar.copy(out=y[:, c * COLS : (c + 1) * COLS], in_=acc[:])
+                else:
+                    nc.vector.tensor_copy(out=y[:, c * COLS : (c + 1) * COLS], in_=acc[:])
             target = window[:].indirect(offsets[:, h * HALF // 16 : (h + 1) * HALF // 16])
             if h == 0:
                 nc.scalar.activation(target, y[:], COPY)

from contextlib import ExitStack

import concourse.mybir as mybir

K, T, N, U = 1024, 512, 128, 1024
FLOPS = 2 * K * T * N

F32 = mybir.dt.float32
BF16 = mybir.dt.bfloat16
I32 = mybir.dt.int32
U32 = mybir.dt.uint32
U16 = mybir.dt.uint16
U8 = mybir.dt.uint8
FP8X4 = mybir.dt.float8_e4m3fn_x4
COPY = mybir.ActivationFunctionType.Copy

P = 128
PACK = 4
K_PASS = P * PACK
PASSES = K // K_PASS
HALF = T // 2
COLS = 128


def tile_picked_wkvput_none_l_kernel(tc, x_words, x_scales, mem, w1, slot, out):
    nc = tc.nc
    with ExitStack() as ctx:
        keep = ctx.enter_context(tc.tile_pool(name="keep", bufs=1))
        psum = ctx.enter_context(tc.psum_pool(name="psum", bufs=1))

        w_raw = []
        for g in range(PASSES):
            raw = keep.tile([P, PACK, N], F32, name="w_raw%d" % g, align_bytes=256)
            nc.sync.dma_start(out=raw[:], in_=w1[g * K_PASS : (g + 1) * K_PASS, :].rearrange("(p j) m -> p j m", j=PACK))
            w_raw.append(raw)

        def load_scales(h, queues):
            plane = keep.tile([P, PASSES, HALF], U8, name="xs%d" % h, align_bytes=256)
            for r in range(4):
                queues[r].dma_start(
                    out=plane[r:P:32, :, :].bitcast(I32),
                    in_=x_scales[:, r:16:4, h * HALF : (h + 1) * HALF].rearrange("z q c -> q z c").bitcast(I32),
                )
            return plane

        xs = [load_scales(0, [nc.scalar, nc.scalar, nc.scalar, nc.sync])]

        words = x_words.rearrange("z p c r -> p z (c r)")
        early = keep.tile([P, PASSES, HALF], U32, name="early", align_bytes=256)
        nc.sync.dma_start(out=early[:].bitcast(I32), in_=words[:, :, 0 : PACK * HALF].bitcast(I32))
        window = keep.tile([P, U], F32, name="window", align_bytes=256)
        nc.sync.dma_start(out=window[:], in_=mem)
        offsets = keep.tile([P, T // 16], U16, name="offsets")
        nc.sync.dma_start(offsets[:], slot)
        xs.append(load_scales(1, [nc.sync] * 4))
        late = []
        for g in range(PASSES):
            t = keep.tile([P, HALF], U32, name="late%d" % g, align_bytes=256)
            nc.sync.dma_start(out=t[:].bitcast(I32), in_=words[:, g, PACK * HALF : PACK * T].bitcast(I32))
            late.append(t)
        x_codes = [[early[:, g, :] for g in range(PASSES)], [late[g][:] for g in range(PASSES)]]

        w_codes, w_scales = [], []
        for g in range(PASSES):
            grouped = keep.tile([P, N, PACK], BF16, name="w_bf%d" % g, align_bytes=256)
            dst = grouped[:].rearrange("p (c i) t -> p c t i", i=4)
            src = w_raw[g][:].rearrange("p t (c i) -> p c t i", i=4)
            nc.vector.tensor_copy(out=dst[:, 0:16], in_=src[:, 0:16])
            nc.scalar.copy(out=dst[:, 16:32], in_=src[:, 16:32])
            codes = keep.tile([P, N], U32, name="w_codes%d" % g, align_bytes=256)
            scales = keep.tile([P, N], U8, name="w_scales%d" % g, align_bytes=256)
            nc.vector.quantize_mx(out=codes[:].bitcast(FP8X4), scales=scales[:], in_=grouped[:].rearrange("p m j -> p (m j)"))
            w_codes.append(codes)
            w_scales.append(scales)

        for h in range(2):
            y = keep.tile([P, HALF], F32, name="y%d" % h, align_bytes=256)
            accs = [psum.tile([P, COLS], F32, name="acc%d_%d" % (h, c)) for c in range(HALF // COLS)]
            for g in range(PASSES):
                for c, acc in enumerate(accs):
                    a = c * COLS
                    nc.tensor.matmul_mx(
                        out=acc[:],
                        lhsT=w_codes[g][:].bitcast(FP8X4),
                        lhsT_scale=w_scales[g][:],
                        rhs=x_codes[h][g][:, a : a + COLS].bitcast(FP8X4),
                        rhs_scale=xs[h][:, g, a : a + COLS],
                        start=(g == 0),
                        stop=(g == PASSES - 1),
                    )
            for c, acc in enumerate(accs):
                if h == 0:
                    nc.scalar.copy(out=y[:, c * COLS : (c + 1) * COLS], in_=acc[:])
                else:
                    nc.vector.tensor_copy(out=y[:, c * COLS : (c + 1) * COLS], in_=acc[:])
            target = window[:].indirect(offsets[:, h * HALF // 16 : (h + 1) * HALF // 16])
            if h == 0:
                nc.scalar.activation(target, y[:], COPY)
            else:
                nc.vector.tensor_copy(target, y[:])

        nc.sync.dma_start(out=out, in_=window[:])
